import numpy as np
import ml_dtypes


def mxq(x, axis, fmt="e4m3"):
    dtype, down = {"e4m3": (ml_dtypes.float8_e4m3fn, 7), "e5m2": (ml_dtypes.float8_e5m2, 14)}[fmt]
    v = np.moveaxis(np.asarray(x, np.float32).astype(ml_dtypes.bfloat16).astype(np.float64), axis, -1)
    blocks = v.reshape(v.shape[:-1] + (-1, 32))
    amax = np.abs(blocks).max(-1, keepdims=True)
    byte = np.maximum(np.where(amax > 0, np.frexp(amax)[1] - 1 + 127, 0) - down, 1)
    scale = np.exp2(byte - 127.0)
    codes = (blocks / scale).astype(np.float32).astype(dtype).astype(np.float64)
    return np.moveaxis((codes * scale).reshape(v.shape), -1, axis)


WIDE = False


def mx_kscale(k):
    if not WIDE:
        return np.ones(k)
    levels = np.array([24, -24, 12, -12, 0])
    if k % 512:
        return np.exp2(np.random.permutation(np.resize(levels, k // 32))).repeat(32)
    a = np.empty((k // 512, 16))
    for p in range(k // 512):
        a[p, :8] = np.random.permutation(np.resize(levels, 8))
        for g in range(8):
            far = levels[np.abs(levels - a[p, g]) >= 10]
            a[p, g + 8] = far[np.random.randint(len(far))]
    return np.exp2(a.ravel()).repeat(32)


def f64(x):
    return np.asarray(x).astype(np.float64)


E2M1 = np.array([0.0, 0.5, 1.0, 1.5, 2.0, 3.0, 4.0, 6.0, -0.0, -0.5, -1.0, -1.5, -2.0, -3.0, -4.0, -6.0])


def pack_weight(w, fmt):
    k, n = w.shape
    w = f64(np.asarray(w, np.float32).astype(ml_dtypes.bfloat16)).reshape(k // 32, 32, n)
    amax = np.abs(w).max(1)
    if fmt == "e4m3":
        byte = np.frexp(amax)[1] - 1 + 127 - 7
    else:
        mant, ex = np.frexp(amax / 6.0)
        byte = np.where(mant > 0.5, ex, ex - 1) + 127
    byte = np.clip(np.where(amax > 0, byte, 1), 1, 254)
    scaled = (w * np.exp2(127.0 - byte)[:, None, :]).reshape(k, n).astype(np.float32)
    by_word = np.ascontiguousarray(scaled.reshape(k // 512, 128, 4, n).transpose(0, 1, 3, 2))
    if fmt == "e4m3":
        words = by_word.astype(ml_dtypes.float8_e4m3fn).view(np.uint8)
    else:
        c = by_word.astype(ml_dtypes.float4_e2m1fn).view(np.uint8) & 0xF
        words = (c[..., 0::2] | (c[..., 1::2] << 4)).reshape(k // 512, 128, 2 * n)
    return np.ascontiguousarray(words), np.ascontiguousarray(byte.astype(np.uint8).reshape(k // 512, 16, n))


def unpack_weight(words, scales, fmt):
    g, _, n = scales.shape
    words = np.ascontiguousarray(words).reshape(g, 128, n, -1)
    if fmt == "e4m3":
        vals = words.view(ml_dtypes.float8_e4m3fn).astype(np.float64)
    else:
        nib = np.empty((g, 128, n, 4), np.uint8)
        nib[..., 0::2] = words & 0xF
        nib[..., 1::2] = words >> 4
        vals = E2M1[nib]
    vals = vals * np.repeat(np.exp2(scales.astype(np.float64) - 127.0), 8, axis=1)[..., None]
    return vals.transpose(0, 1, 3, 2).reshape(g * 512, n)


K, F, T = 1024, 1024, 1536


def setup_inputs():
    n = np.random.standard_normal
    s = mx_kscale(K)[:, None]
    v = n((K, F)) / np.sqrt(K)
    p_v4 = pack_weight(v / s, "e2m1")
    p_vs = pack_weight(v ** 2 / s ** 2, "e4m3")
    return {
        "x": (n((K, T)) * s).astype(np.float32),
        "v4_words": p_v4[0],
        "v4_scales": p_v4[1],
        "vs_words": p_vs[0],
        "vs_scales": p_vs[1],
        "g": (np.random.uniform(0.5, 1.5, F)).astype(np.float32),
    }


def reference(x, v4_words, v4_scales, vs_words, vs_scales, g):
    x_ = mxq(f64(x), 0, "e4m3")
    xs_ = mxq(f64(x) * f64(x), 0, "e4m3")
    v4_ = unpack_weight(v4_words, v4_scales, "e2m1")
    vs_ = unpack_weight(vs_words, vs_scales, "e4m3")
    a = v4_.T @ x_
    c = vs_.T @ xs_
    return 0.5 * (a * a - c) * f64(g)[:, None]

@@ -1,0 +1,270 @@
+from contextlib import ExitStack
+
+import concourse.mybir as mybir
+from concourse.masks import make_identity
+
+K, F, T = 1024, 1024, 1536
+FLOPS = 2 * 2 * K * F * T
+
+F32 = mybir.dt.float32
+BF16 = mybir.dt.bfloat16
+I32 = mybir.dt.int32
+U32 = mybir.dt.uint32
+U8 = mybir.dt.uint8
+FP8X4 = mybir.dt.float8_e4m3fn_x4
+FP4X4 = mybir.dt.float4_e2m1fn_x4
+ALU = mybir.AluOpType
+ACT = mybir.ActivationFunctionType
+
+P = 128
+PACK = 4
+K_PASS = P * PACK
+PASSES = K // K_PASS
+N_TILE = 512
+T_TILES = T // N_TILE
+F_TILES = F // P
+STEPS = T_TILES * F_TILES
+PIECE = 256
+RUN = 2
+VS_ROW = 4
+EARLY = "VVS"
+LATE = "V"
+SWITCH = 16
+OPEN_AHEAD = 2
+
+
+def tile_mix_fm_wgt_kernel(tc, x, v4_words, v4_scales, vs_words, vs_scales, g, out):
+    nc = tc.nc
+    with ExitStack() as ctx:
+        keep = ctx.enter_context(tc.tile_pool(name="keep", bufs=1))
+        stage = ctx.enter_context(tc.tile_pool(name="stage", bufs=4))
+        results = ctx.enter_context(tc.tile_pool(name="results", bufs=STEPS))
+        psum_a = ctx.enter_context(tc.psum_pool(name="psum_a", bufs=4))
+        psum_c = ctx.enter_context(tc.psum_pool(name="psum_c", bufs=4))
+        ctx.enter_context(tc.manual_schedule())
+
+        g_rows = keep.tile([P, P], F32, name="g_rows")
+        ident = keep.tile([P, P], F32, name="ident")
+        half_g = keep.tile([P, F_TILES], F32, name="half_g")
+        v4_plane = keep.tile([P, PASSES * F], U8, name="v4_plane", align_bytes=64)
+        vs_plane = keep.tile([P, PASSES * F], U8, name="vs_plane", align_bytes=64)
+
+        nc.gpsimd.memset(g_rows[:], 0.0)
+        nc.vector.memset(v4_plane[:].bitcast(U32), 0)
+        nc.vector.memset(vs_plane[:].bitcast(U32), 0)
+        make_identity(nc, ident[:])
+
+        def load_scales(queue, plane, first_row, scales):
+            for q in range(4):
+                rows = plane[32 * q + first_row : 32 * q + first_row + 4, :]
+                queue.dma_start(
+                    out=rows.bitcast(I32).rearrange("r (a n) -> r a n", a=PASSES),
+                    in_=scales[:, 4 * q : 4 * q + 4, :].rearrange("a r n -> r a n").bitcast(I32),
+                )
+
+        nc.scalar.dma_start(out=g_rows[0:F_TILES, :], in_=g.rearrange("(c p) -> c p", p=P))
+        load_scales(nc.scalar, v4_plane, 0, v4_scales)
+
+        raw = {}
+
+        def load_x(tt, a, c0, width):
+            tile = keep.tile([P, PACK, width], F32, name=f"raw_{tt}_{a}_{c0}")
+            t0 = tt * N_TILE + c0
+            rows = x[a * K_PASS : (a + 1) * K_PASS, t0 : t0 + width]
+            nc.sync.dma_start(out=tile[:], in_=rows.rearrange("(p j) w -> p j w", j=PACK))
+            for c in range(0, width, PIECE):
+                raw[(tt, a, c0 + c)] = tile[:, :, c : c + PIECE]
+
+        v4_codes = {}
+        vs_codes = {}
+
+        def load_v4(f0, f1):
+            tile = keep.tile([P, PASSES, 2 * P * (f1 - f0)], U8, name=f"v4_{f0}", align_bytes=64)
+            src = v4_words[:, :, 2 * P * f0 : 2 * P * f1].rearrange("a p n -> p a n")
+            nc.sync.dma_start(out=tile[:].bitcast(I32), in_=src.bitcast(I32))
+            for f in range(f0, f1):
+                for a in range(PASSES):
+                    v4_codes[(a, f)] = tile[:, a, 2 * P * (f - f0) : 2 * P * (f - f0 + 1)]
+
+        def load_vs(f0, f1):
+            tile = keep.tile([P, PASSES, P * (f1 - f0)], U32, name=f"vs_{f0}", align_bytes=64)
+            src = vs_words.rearrange("a p n t -> p a (n t)")[:, :, 4 * P * f0 : 4 * P * f1]
+            nc.sync.dma_start(out=tile[:].bitcast(I32), in_=src.bitcast(I32))
+            for f in range(f0, f1):
+                for a in range(PASSES):
+                    vs_codes[(a, f)] = tile[:, a, P * (f - f0) : P * (f - f0 + 1)]
+
+        load_x(0, 0, 0, PIECE)
+        load_x(0, 0, PIECE, PIECE)
+        load_x(0, 1, 0, N_TILE)
+        load_scales(nc.sync, vs_plane, VS_ROW, vs_scales)
+        load_v4(0, F_TILES)
+        load_vs(0, 2)
+        load_x(1, 0, 0, PIECE)
+        load_vs(2, 4)
+        load_x(1, 0, PIECE, PIECE)
+        load_vs(4, F_TILES)
+        load_x(1, 1, 0, N_TILE)
+        load_x(2, 0, 0, N_TILE)
+        load_x(2, 1, 0, N_TILE)
+
+        g_cols = psum_a.tile([P, N_TILE], F32, name="a_sum")
+        nc.tensor.transpose(g_cols[:, 0:P], g_rows[:], ident[:])
+        nc.vector.tensor_scalar(out=half_g[:], in0=g_cols[:, 0:F_TILES], scalar1=0.5, scalar2=None, op0=ALU.mult)
+
+        codes = {}
+        planes = {}
+        for name in ("x", "xs"):
+            for tt in range(T_TILES):
+                for a in range(PASSES):
+                    codes[(name, tt, a)] = keep.tile([P, N_TILE], U32, name=f"codes_{name}_{tt}_{a}", align_bytes=64)
+                    planes[(name, tt, a)] = keep.tile([P, N_TILE], U8, name=f"plane_{name}_{tt}_{a}", align_bytes=64)
+
+        rounded = {}
+
+        def views(piece, tile):
+            dst = tile[:].rearrange("p (c i j) -> p c j i", i=RUN, j=PACK)
+            src = raw[piece].rearrange("p j (c i) -> p c j i", i=RUN)
+            return dst, src
+
+        def round_x(piece):
+            tile = stage.tile([P, PACK * PIECE], BF16, name="x_bf16", align_bytes=64)
+            dst, src = views(piece, tile)
+            nc.vector.tensor_copy(out=dst, in_=src)
+            rounded[("x", piece)] = tile
+
+        def round_xs(piece):
+            tile = stage.tile([P, PACK * PIECE], BF16, name="xs_bf16", align_bytes=64)
+            dst, src = views(piece, tile)
+            nc.scalar.activation(out=dst, in_=src, func=ACT.Square)
+            rounded[("xs", piece)] = tile
+
+        def quantize(name, piece):
+            tt, a, c0 = piece
+            nc.vector.quantize_mx(
+                out=codes[(name, tt, a)][:, c0 : c0 + PIECE].bitcast(FP8X4),
+                scales=planes[(name, tt, a)][:, c0 : c0 + PIECE],
+                in_=rounded[(name, piece)][:],
+            )
+
+        a_sums = {}
+        c_sums = {}
+
+        def pass_a(step, a):
+            tt, f = divmod(step, F_TILES)
+            if a == 0:
+                a_sums[step] = psum_a.tile([P, N_TILE], F32, name="a_sum")
+            nc.tensor.matmul_mx(
+                out=a_sums[step][:],
+                lhsT=v4_codes[(a, f)].bitcast(FP4X4),
+                lhsT_scale=v4_plane[:, a * F + f * P : a * F + (f + 1) * P],
+                rhs=codes[("x", tt, a)][:].bitcast(FP8X4),
+                rhs_scale=planes[("x", tt, a)][:],
+                start=(a == 0),
+                stop=(a == PASSES - 1),
+            )
+
+        def pass_c(step, a):
+            tt, f = divmod(step, F_TILES)
+            if a == 0:
+                c_sums[step] = psum_c.tile([P, N_TILE], F32, name="c_sum")
+            nc.tensor.matmul_mx(
+                out=c_sums[step][:],
+                lhsT=vs_codes[(a, f)].bitcast(FP8X4),
+                lhsT_scale=vs_plane[VS_ROW:P, a * F + f * P : a * F + (f + 1) * P],
+                rhs=codes[("xs", tt, a)][:].bitcast(FP8X4),
+                rhs_scale=planes[("xs", tt, a)][:],
+                start=(a == 0),
+                stop=(a == PASSES - 1),
+            )
+
+        squares = {}
+        diffs = {}
+
+        def square_a(step, cols):
+            if step not in squares:
+                squares[step] = stage.tile([P, N_TILE], F32, name="a_squared")
+            nc.scalar.activation(out=squares[step][:, cols], in_=a_sums[step][:, cols], func=ACT.Square)
+
+        def subtract_c(step, cols):
+            if step not in diffs:
+                diffs[step] = results.tile([P, N_TILE], F32, name="diff", bufs=8)
+            nc.vector.tensor_tensor(
+                out=diffs[step][:, cols], in0=squares[step][:, cols], in1=c_sums[step][:, cols], op=ALU.subtract
+            )
+
+        def weigh_and_store(step, cols, engine):
+            tt, f = divmod(step, F_TILES)
+            width = cols.stop - cols.start
+            result = results.tile([P, width], F32, name="result", bufs=STEPS + 1)
+            weight = half_g[:, f : f + 1]
+            if engine == "V":
+                nc.vector.tensor_scalar(
+                    out=result[:], in0=diffs[step][:, cols], scalar1=weight, scalar2=None, op0=ALU.mult
+                )
+            elif engine == "S":
+                nc.scalar.activation(out=result[:], in_=diffs[step][:, cols], func=ACT.Copy, scale=weight)
+            else:
+                nc.gpsimd.tensor_scalar(
+                    out=result[:], in0=diffs[step][:, cols], scalar1=weight, scalar2=0.0, op0=ALU.mult, op1=ALU.add
+                )
+            t0 = tt * N_TILE
+            nc.sync.dma_start(out=out[f * P : (f + 1) * P, t0 + cols.start : t0 + cols.stop], in_=result[:])
+
+        for a in range(PASSES):
+            pieces = [(0, a, c0) for c0 in range(0, N_TILE, PIECE)]
+            for piece in pieces:
+                round_xs(piece)
+                round_x(piece)
+            for name in ("x", "xs"):
+                for piece in pieces:
+                    quantize(name, piece)
+
+        later = [(tt, a, c0) for tt in range(1, T_TILES) for a in range(PASSES) for c0 in range(0, N_TILE, PIECE)]
+        due = {}
+        for j, piece in enumerate(later):
+            due.setdefault(1 + j * 8 // 5, []).append(piece)
+
+        whole = slice(0, N_TILE)
+        halves = [slice(0, N_TILE // 2), slice(N_TILE // 2, N_TILE)]
+        stored = 0
+        previous = []
+        for step in range(STEPS):
+            if step > 0 and step % F_TILES == 0:
+                for ahead in range(OPEN_AHEAD):
+                    pass_a(step + ahead, 0)
+                    pass_c(step + ahead, 0)
+            if step not in a_sums:
+                pass_a(step, 0)
+            pass_a(step, 1)
+            if step not in c_sums:
+                pass_c(step, 0)
+            pass_c(step, 1)
+            if step == STEPS - 1:
+                break
+            current = due.get(step, [])
+            square_a(step, whole)
+            for piece in current:
+                round_xs(piece)
+            subtract_c(step, whole)
+            for name in ("x", "xs"):
+                for piece in previous:
+                    quantize(name, piece)
+            engines = EARLY[step % len(EARLY)] if step < SWITCH else LATE
+            for engine in engines:
+                if stored < step:
+                    weigh_and_store(stored, whole, engine)
+                    stored = stored + 1
+            for piece in current:
+                round_x(piece)
+            previous = current
+
+        last = STEPS - 1
+        for cols in halves:
+            square_a(last, cols)
+        for step in range(stored, last):
+            weigh_and_store(step, whole, LATE[step % len(LATE)])
+        for cols in halves:
+            subtract_c(last, cols)
+        for cols in halves:
+            weigh_and_store(last, cols, "V")

@@ -27,7 +27,7 @@ STEPS = T_TILES * F_TILES
 PIECE = 256
 RUN = 2
 VS_ROW = 4
-EARLY = "VVS"
+EARLY = "G"
 LATE = "V"
 SWITCH = 16
 OPEN_AHEAD = 2
@@ -62,8 +62,6 @@ def tile_mix_fm_wgt_kernel(tc, x, v4_words, v4_scales, vs_words, vs_scales, g, o
                     in_=scales[:, 4 * q : 4 * q + 4, :].rearrange("a r n -> r a n").bitcast(I32),
                 )
 
-        nc.scalar.dma_start(out=g_rows[0:F_TILES, :], in_=g.rearrange("(c p) -> c p", p=P))
-        load_scales(nc.scalar, v4_plane, 0, v4_scales)
 
         raw = {}
 
@@ -96,21 +94,22 @@ def tile_mix_fm_wgt_kernel(tc, x, v4_words, v4_scales, vs_words, vs_scales, g, o
 
         load_x(0, 0, 0, PIECE)
         load_x(0, 0, PIECE, PIECE)
+        nc.sync.dma_start(out=g_rows[0:F_TILES, :], in_=g.rearrange("(c p) -> c p", p=P))
+        load_scales(nc.sync, v4_plane, 0, v4_scales)
         load_x(0, 1, 0, N_TILE)
-        load_scales(nc.sync, vs_plane, VS_ROW, vs_scales)
-        load_v4(0, F_TILES)
+        load_v4(0, 8)
         load_vs(0, 2)
+        load_scales(nc.sync, vs_plane, VS_ROW, vs_scales)
         load_x(1, 0, 0, PIECE)
         load_vs(2, 4)
         load_x(1, 0, PIECE, PIECE)
-        load_vs(4, F_TILES)
+        load_vs(4, 8)
         load_x(1, 1, 0, N_TILE)
         load_x(2, 0, 0, N_TILE)
         load_x(2, 1, 0, N_TILE)
 
         g_cols = psum_a.tile([P, N_TILE], F32, name="a_sum")
         nc.tensor.transpose(g_cols[:, 0:P], g_rows[:], ident[:])
-        nc.vector.tensor_scalar(out=half_g[:], in0=g_cols[:, 0:F_TILES], scalar1=0.5, scalar2=None, op0=ALU.mult)
 
         codes = {}
         planes = {}
@@ -219,6 +218,8 @@ def tile_mix_fm_wgt_kernel(tc, x, v4_words, v4_scales, vs_words, vs_scales, g, o
             for name in ("x", "xs"):
                 for piece in pieces:
                     quantize(name, piece)
+
+        nc.vector.tensor_scalar(out=half_g[:], in0=g_cols[:, 0:F_TILES], scalar1=0.5, scalar2=None, op0=ALU.mult)
 
         later = [(tt, a, c0) for tt in range(1, T_TILES) for a in range(PASSES) for c0 in range(0, N_TILE, PIECE)]
         due = {}

@@ -25,12 +25,14 @@ T_TILES = T // N_TILE
 F_TILES = F // P
 STEPS = T_TILES * F_TILES
 PIECE = 256
-RUN = 2
+LATER_PIECE = 512
+LAG = 1
+RUN = 4
 VS_ROW = 4
-EARLY = "G"
-LATE = "V"
+EARLY = "SV"
+LATE = "SV"
 SWITCH = 16
-OPEN_AHEAD = 2
+OPEN_AHEAD = 0
 
 
 def tile_mix_fm_wgt_kernel(tc, x, v4_words, v4_scales, vs_words, vs_scales, g, out):
@@ -70,8 +72,9 @@ def tile_mix_fm_wgt_kernel(tc, x, v4_words, v4_scales, vs_words, vs_scales, g, o
             t0 = tt * N_TILE + c0
             rows = x[a * K_PASS : (a + 1) * K_PASS, t0 : t0 + width]
             nc.sync.dma_start(out=tile[:], in_=rows.rearrange("(p j) w -> p j w", j=PACK))
-            for c in range(0, width, PIECE):
-                raw[(tt, a, c0 + c)] = tile[:, :, c : c + PIECE]
+            piece = PIECE if tt == 0 else LATER_PIECE
+            for c in range(0, width, piece):
+                raw[(tt, a, c0 + c)] = tile[:, :, c : c + piece]
 
         v4_codes = {}
         vs_codes = {}
@@ -97,12 +100,11 @@ def tile_mix_fm_wgt_kernel(tc, x, v4_words, v4_scales, vs_words, vs_scales, g, o
         nc.sync.dma_start(out=g_rows[0:F_TILES, :], in_=g.rearrange("(c p) -> c p", p=P))
         load_scales(nc.sync, v4_plane, 0, v4_scales)
         load_x(0, 1, 0, N_TILE)
-        load_v4(0, 8)
-        load_vs(0, 2)
+        load_v4(0, 4)
+        load_vs(0, 4)
         load_scales(nc.sync, vs_plane, VS_ROW, vs_scales)
-        load_x(1, 0, 0, PIECE)
-        load_vs(2, 4)
-        load_x(1, 0, PIECE, PIECE)
+        load_x(1, 0, 0, N_TILE)
+        load_v4(4, 8)
         load_vs(4, 8)
         load_x(1, 1, 0, N_TILE)
         load_x(2, 0, 0, N_TILE)
@@ -127,22 +129,23 @@ def tile_mix_fm_wgt_kernel(tc, x, v4_words, v4_scales, vs_words, vs_scales, g, o
             return dst, src
 
         def round_x(piece):
-            tile = stage.tile([P, PACK * PIECE], BF16, name="x_bf16", align_bytes=64)
+            tile = stage.tile([P, PACK * raw[piece].shape[2]], BF16, name="x_bf16", align_bytes=64)
             dst, src = views(piece, tile)
             nc.vector.tensor_copy(out=dst, in_=src)
             rounded[("x", piece)] = tile
 
         def round_xs(piece):
-            tile = stage.tile([P, PACK * PIECE], BF16, name="xs_bf16", align_bytes=64)
+            tile = stage.tile([P, PACK * raw[piece].shape[2]], BF16, name="xs_bf16", align_bytes=64)
             dst, src = views(piece, tile)
             nc.scalar.activation(out=dst, in_=src, func=ACT.Square)
             rounded[("xs", piece)] = tile
 
         def quantize(name, piece):
             tt, a, c0 = piece
+            width = raw[piece].shape[2]
             nc.vector.quantize_mx(
-                out=codes[(name, tt, a)][:, c0 : c0 + PIECE].bitcast(FP8X4),
-                scales=planes[(name, tt, a)][:, c0 : c0 + PIECE],
+                out=codes[(name, tt, a)][:, c0 : c0 + width].bitcast(FP8X4),
+                scales=planes[(name, tt, a)][:, c0 : c0 + width],
                 in_=rounded[(name, piece)][:],
             )
 
@@ -221,10 +224,10 @@ def tile_mix_fm_wgt_kernel(tc, x, v4_words, v4_scales, vs_words, vs_scales, g, o
 
         nc.vector.tensor_scalar(out=half_g[:], in0=g_cols[:, 0:F_TILES], scalar1=0.5, scalar2=None, op0=ALU.mult)
 
-        later = [(tt, a, c0) for tt in range(1, T_TILES) for a in range(PASSES) for c0 in range(0, N_TILE, PIECE)]
+        later = [(tt, a, c0) for tt in range(1, T_TILES) for a in range(PASSES) for c0 in range(0, N_TILE, LATER_PIECE)]
         due = {}
         for j, piece in enumerate(later):
-            due.setdefault(1 + j * 8 // 5, []).append(piece)
+            due.setdefault(1 + j * 17 // 5, []).append(piece)
 
         whole = slice(0, N_TILE)
         halves = [slice(0, N_TILE // 2), slice(N_TILE // 2, N_TILE)]
@@ -251,9 +254,9 @@ def tile_mix_fm_wgt_kernel(tc, x, v4_words, v4_scales, vs_words, vs_scales, g, o
             for name in ("x", "xs"):
                 for piece in previous:
                     quantize(name, piece)
-            engines = EARLY[step % len(EARLY)] if step < SWITCH else LATE
+            engines = EARLY[step % len(EARLY)] if step < SWITCH else LATE[step % len(LATE)]
             for engine in engines:
-                if stored < step:
+                if stored < step - LAG:
                     weigh_and_store(stored, whole, engine)
                     stored = stored + 1
             for piece in current:
@@ -264,7 +267,7 @@ def tile_mix_fm_wgt_kernel(tc, x, v4_words, v4_scales, vs_words, vs_scales, g, o
         for cols in halves:
             square_a(last, cols)
         for step in range(stored, last):
-            weigh_and_store(step, whole, LATE[step % len(LATE)])
+            weigh_and_store(step, whole, "V")
         for cols in halves:
             subtract_c(last, cols)
         for cols in halves:

@@ -25,14 +25,14 @@ T_TILES = T // N_TILE
 F_TILES = F // P
 STEPS = T_TILES * F_TILES
 PIECE = 256
-LATER_PIECE = 512
-LAG = 1
+LATER_PIECE = 256
+LAG = 0
 RUN = 4
 VS_ROW = 4
-EARLY = "SV"
-LATE = "SV"
+EARLY = "G"
+LATE = "G"
 SWITCH = 16
-OPEN_AHEAD = 0
+OPEN_AHEAD = 2
 
 
 def tile_mix_fm_wgt_kernel(tc, x, v4_words, v4_scales, vs_words, vs_scales, g, out):
@@ -227,7 +227,7 @@ def tile_mix_fm_wgt_kernel(tc, x, v4_words, v4_scales, vs_words, vs_scales, g, o
         later = [(tt, a, c0) for tt in range(1, T_TILES) for a in range(PASSES) for c0 in range(0, N_TILE, LATER_PIECE)]
         due = {}
         for j, piece in enumerate(later):
-            due.setdefault(1 + j * 17 // 5, []).append(piece)
+            due.setdefault(1 + j * 8 // 5, []).append(piece)
 
         whole = slice(0, N_TILE)
         halves = [slice(0, N_TILE // 2), slice(N_TILE // 2, N_TILE)]

@@ -20,18 +20,21 @@ P = 128
 PACK = 4
 K_PASS = P * PACK
 PASSES = K // K_PASS
-N_TILE = 512
-T_TILES = T // N_TILE
+T_TILE = 512
+T_TILES = T // T_TILE
 F_TILES = F // P
 STEPS = T_TILES * F_TILES
 PIECE = 256
-LATER_PIECE = 256
-LAG = 0
 RUN = 4
-VS_ROW = 4
-EARLY = "G"
-LATE = "G"
-SWITCH = 16
+QUADRANT = 32
+SCALE_ROWS = 4
+FP4_BYTES = 2
+FP8_BYTES = 4
+VS_FIRST_ROW = 4
+PSUM_BANKS = 4
+STAGE_BUFS = 4
+DIFF_BUFS = 8
+PIECE_PACE = (9, 5)
 OPEN_AHEAD = 2
 
 
@@ -39,10 +42,10 @@ def tile_mix_fm_wgt_kernel(tc, x, v4_words, v4_scales, vs_words, vs_scales, g, o
     nc = tc.nc
     with ExitStack() as ctx:
         keep = ctx.enter_context(tc.tile_pool(name="keep", bufs=1))
-        stage = ctx.enter_context(tc.tile_pool(name="stage", bufs=4))
-        results = ctx.enter_context(tc.tile_pool(name="results", bufs=STEPS))
-        psum_a = ctx.enter_context(tc.psum_pool(name="psum_a", bufs=4))
-        psum_c = ctx.enter_context(tc.psum_pool(name="psum_c", bufs=4))
+        stage = ctx.enter_context(tc.tile_pool(name="stage", bufs=STAGE_BUFS))
+        results = ctx.enter_context(tc.tile_pool(name="results", bufs=STEPS + 1))
+        psum_a = ctx.enter_context(tc.psum_pool(name="psum_a", bufs=PSUM_BANKS))
+        psum_c = ctx.enter_context(tc.psum_pool(name="psum_c", bufs=PSUM_BANKS))
         ctx.enter_context(tc.manual_schedule())
 
         g_rows = keep.tile([P, P], F32, name="g_rows")
@@ -56,184 +59,134 @@ def tile_mix_fm_wgt_kernel(tc, x, v4_words, v4_scales, vs_words, vs_scales, g, o
         nc.vector.memset(vs_plane[:].bitcast(U32), 0)
         make_identity(nc, ident[:])
 
-        def load_scales(queue, plane, first_row, scales):
-            for q in range(4):
-                rows = plane[32 * q + first_row : 32 * q + first_row + 4, :]
-                queue.dma_start(
-                    out=rows.bitcast(I32).rearrange("r (a n) -> r a n", a=PASSES),
-                    in_=scales[:, 4 * q : 4 * q + 4, :].rearrange("a r n -> r a n").bitcast(I32),
-                )
-
-
         raw = {}
-
-        def load_x(tt, a, c0, width):
-            tile = keep.tile([P, PACK, width], F32, name=f"raw_{tt}_{a}_{c0}")
-            t0 = tt * N_TILE + c0
-            rows = x[a * K_PASS : (a + 1) * K_PASS, t0 : t0 + width]
-            nc.sync.dma_start(out=tile[:], in_=rows.rearrange("(p j) w -> p j w", j=PACK))
-            piece = PIECE if tt == 0 else LATER_PIECE
-            for c in range(0, width, piece):
-                raw[(tt, a, c0 + c)] = tile[:, :, c : c + piece]
-
         v4_codes = {}
         vs_codes = {}
 
+        def load_scales(plane, first_row, scales):
+            for r in range(SCALE_ROWS):
+                rows = plane[first_row + r : P : QUADRANT, :]
+                source = scales[:, r : K_PASS // 32 : SCALE_ROWS, :].rearrange("n q f -> q n f")
+                nc.sync.dma_start(
+                    out=rows.bitcast(I32).rearrange("q (n f) -> q n f", n=PASSES),
+                    in_=source.bitcast(I32),
+                )
+
+        def load_x(tt, n, c0, width):
+            tile = keep.tile([P, PACK, width], F32, name=f"raw_{tt}_{n}_{c0}")
+            t0 = tt * T_TILE + c0
+            rows = x[n * K_PASS : (n + 1) * K_PASS, t0 : t0 + width]
+            nc.sync.dma_start(out=tile[:], in_=rows.rearrange("(p j) w -> p j w", j=PACK))
+            for c in range(0, width, PIECE):
+                raw[(tt, n, c0 + c)] = tile[:, :, c : c + PIECE]
+
         def load_v4(f0, f1):
-            tile = keep.tile([P, PASSES, 2 * P * (f1 - f0)], U8, name=f"v4_{f0}", align_bytes=64)
-            src = v4_words[:, :, 2 * P * f0 : 2 * P * f1].rearrange("a p n -> p a n")
-            nc.sync.dma_start(out=tile[:].bitcast(I32), in_=src.bitcast(I32))
+            row = FP4_BYTES * P
+            tile = keep.tile([P, PASSES, row * (f1 - f0)], U8, name=f"v4_{f0}", align_bytes=64)
+            source = v4_words[:, :, row * f0 : row * f1].rearrange("n p b -> p n b")
+            nc.sync.dma_start(out=tile[:].bitcast(I32), in_=source.bitcast(I32))
             for f in range(f0, f1):
-                for a in range(PASSES):
-                    v4_codes[(a, f)] = tile[:, a, 2 * P * (f - f0) : 2 * P * (f - f0 + 1)]
+                for n in range(PASSES):
+                    v4_codes[(n, f)] = tile[:, n, row * (f - f0) : row * (f - f0 + 1)]
 
         def load_vs(f0, f1):
+            row = FP8_BYTES * P
             tile = keep.tile([P, PASSES, P * (f1 - f0)], U32, name=f"vs_{f0}", align_bytes=64)
-            src = vs_words.rearrange("a p n t -> p a (n t)")[:, :, 4 * P * f0 : 4 * P * f1]
-            nc.sync.dma_start(out=tile[:].bitcast(I32), in_=src.bitcast(I32))
+            source = vs_words.rearrange("n p f j -> p n (f j)")[:, :, row * f0 : row * f1]
+            nc.sync.dma_start(out=tile[:].bitcast(I32), in_=source.bitcast(I32))
             for f in range(f0, f1):
-                for a in range(PASSES):
-                    vs_codes[(a, f)] = tile[:, a, P * (f - f0) : P * (f - f0 + 1)]
+                for n in range(PASSES):
+                    vs_codes[(n, f)] = tile[:, n, P * (f - f0) : P * (f - f0 + 1)]
 
-        load_x(0, 0, 0, PIECE)
-        load_x(0, 0, PIECE, PIECE)
+        load_x(0, 0, 0, T_TILE)
+        load_x(0, 1, 0, T_TILE)
         nc.sync.dma_start(out=g_rows[0:F_TILES, :], in_=g.rearrange("(c p) -> c p", p=P))
-        load_scales(nc.sync, v4_plane, 0, v4_scales)
-        load_x(0, 1, 0, N_TILE)
+        load_scales(v4_plane, 0, v4_scales)
         load_v4(0, 4)
         load_vs(0, 4)
-        load_scales(nc.sync, vs_plane, VS_ROW, vs_scales)
-        load_x(1, 0, 0, N_TILE)
+        load_scales(vs_plane, VS_FIRST_ROW, vs_scales)
+        load_x(1, 0, 0, PIECE)
+        load_x(1, 0, PIECE, PIECE)
         load_v4(4, 8)
-        load_vs(4, 8)
-        load_x(1, 1, 0, N_TILE)
-        load_x(2, 0, 0, N_TILE)
-        load_x(2, 1, 0, N_TILE)
+        load_vs(4, 6)
+        load_x(1, 1, 0, PIECE)
+        load_vs(6, 8)
+        load_x(1, 1, PIECE, PIECE)
+        load_x(2, 0, 0, T_TILE)
+        load_x(2, 1, 0, T_TILE)
 
-        g_cols = psum_a.tile([P, N_TILE], F32, name="a_sum")
+        g_cols = psum_a.tile([P, T_TILE], F32, name="a_sum")
         nc.tensor.transpose(g_cols[:, 0:P], g_rows[:], ident[:])
 
         codes = {}
         planes = {}
         for name in ("x", "xs"):
             for tt in range(T_TILES):
-                for a in range(PASSES):
-                    codes[(name, tt, a)] = keep.tile([P, N_TILE], U32, name=f"codes_{name}_{tt}_{a}", align_bytes=64)
-                    planes[(name, tt, a)] = keep.tile([P, N_TILE], U8, name=f"plane_{name}_{tt}_{a}", align_bytes=64)
+                for n in range(PASSES):
+                    codes[(name, tt, n)] = keep.tile([P, T_TILE], U32, name=f"codes_{name}_{tt}_{n}", align_bytes=64)
+                    planes[(name, tt, n)] = keep.tile([P, T_TILE], U8, name=f"plane_{name}_{tt}_{n}", align_bytes=64)
 
         rounded = {}
 
-        def views(piece, tile):
+        def interleaved(piece, tile):
             dst = tile[:].rearrange("p (c i j) -> p c j i", i=RUN, j=PACK)
             src = raw[piece].rearrange("p j (c i) -> p c j i", i=RUN)
             return dst, src
 
         def round_x(piece):
-            tile = stage.tile([P, PACK * raw[piece].shape[2]], BF16, name="x_bf16", align_bytes=64)
-            dst, src = views(piece, tile)
+            tile = stage.tile([P, PACK * PIECE], BF16, name="x_bf16", align_bytes=64)
+            dst, src = interleaved(piece, tile)
             nc.vector.tensor_copy(out=dst, in_=src)
             rounded[("x", piece)] = tile
 
         def round_xs(piece):
-            tile = stage.tile([P, PACK * raw[piece].shape[2]], BF16, name="xs_bf16", align_bytes=64)
-            dst, src = views(piece, tile)
+            tile = stage.tile([P, PACK * PIECE], BF16, name="xs_bf16", align_bytes=64)
+            dst, src = interleaved(piece, tile)
             nc.scalar.activation(out=dst, in_=src, func=ACT.Square)
             rounded[("xs", piece)] = tile
 
-        def quantize(name, piece):
-            tt, a, c0 = piece
-            width = raw[piece].shape[2]
-            nc.vector.quantize_mx(
-                out=codes[(name, tt, a)][:, c0 : c0 + width].bitcast(FP8X4),
-                scales=planes[(name, tt, a)][:, c0 : c0 + width],
-                in_=rounded[(name, piece)][:],
-            )
+        def quantize(pieces):
+            for name in ("x", "xs"):
+                for piece in pieces:
+                    tt, n, c0 = piece
+                    nc.vector.quantize_mx(
+                        out=codes[(name, tt, n)][:, c0 : c0 + PIECE].bitcast(FP8X4),
+                        scales=planes[(name, tt, n)][:, c0 : c0 + PIECE],
+                        in_=rounded[(name, piece)][:],
+                    )
 
         a_sums = {}
         c_sums = {}
 
-        def pass_a(step, a):
+        def pass_a(step, n):
             tt, f = divmod(step, F_TILES)
-            if a == 0:
-                a_sums[step] = psum_a.tile([P, N_TILE], F32, name="a_sum")
+            if n == 0:
+                a_sums[step] = psum_a.tile([P, T_TILE], F32, name="a_sum")
             nc.tensor.matmul_mx(
                 out=a_sums[step][:],
-                lhsT=v4_codes[(a, f)].bitcast(FP4X4),
-                lhsT_scale=v4_plane[:, a * F + f * P : a * F + (f + 1) * P],
-                rhs=codes[("x", tt, a)][:].bitcast(FP8X4),
-                rhs_scale=planes[("x", tt, a)][:],
-                start=(a == 0),
-                stop=(a == PASSES - 1),
+                lhsT=v4_codes[(n, f)].bitcast(FP4X4),
+                lhsT_scale=v4_plane[:, n * F + f * P : n * F + (f + 1) * P],
+                rhs=codes[("x", tt, n)][:].bitcast(FP8X4),
+                rhs_scale=planes[("x", tt, n)][:],
+                start=(n == 0),
+                stop=(n == PASSES - 1),
             )
 
-        def pass_c(step, a):
+        def pass_c(step, n):
             tt, f = divmod(step, F_TILES)
-            if a == 0:
-                c_sums[step] = psum_c.tile([P, N_TILE], F32, name="c_sum")
+            if n == 0:
+                c_sums[step] = psum_c.tile([P, T_TILE], F32, name="c_sum")
             nc.tensor.matmul_mx(
                 out=c_sums[step][:],
-                lhsT=vs_codes[(a, f)].bitcast(FP8X4),
-                lhsT_scale=vs_plane[VS_ROW:P, a * F + f * P : a * F + (f + 1) * P],
-                rhs=codes[("xs", tt, a)][:].bitcast(FP8X4),
-                rhs_scale=planes[("xs", tt, a)][:],
-                start=(a == 0),
-                stop=(a == PASSES - 1),
+                lhsT=vs_codes[(n, f)].bitcast(FP8X4),
+                lhsT_scale=vs_plane[VS_FIRST_ROW:P, n * F + f * P : n * F + (f + 1) * P],
+                rhs=codes[("xs", tt, n)][:].bitcast(FP8X4),
+                rhs_scale=planes[("xs", tt, n)][:],
+                start=(n == 0),
+                stop=(n == PASSES - 1),
             )
 
-        squares = {}
-        diffs = {}
-
-        def square_a(step, cols):
-            if step not in squares:
-                squares[step] = stage.tile([P, N_TILE], F32, name="a_squared")
-            nc.scalar.activation(out=squares[step][:, cols], in_=a_sums[step][:, cols], func=ACT.Square)
-
-        def subtract_c(step, cols):
-            if step not in diffs:
-                diffs[step] = results.tile([P, N_TILE], F32, name="diff", bufs=8)
-            nc.vector.tensor_tensor(
-                out=diffs[step][:, cols], in0=squares[step][:, cols], in1=c_sums[step][:, cols], op=ALU.subtract
-            )
-
-        def weigh_and_store(step, cols, engine):
-            tt, f = divmod(step, F_TILES)
-            width = cols.stop - cols.start
-            result = results.tile([P, width], F32, name="result", bufs=STEPS + 1)
-            weight = half_g[:, f : f + 1]
-            if engine == "V":
-                nc.vector.tensor_scalar(
-                    out=result[:], in0=diffs[step][:, cols], scalar1=weight, scalar2=None, op0=ALU.mult
-                )
-            elif engine == "S":
-                nc.scalar.activation(out=result[:], in_=diffs[step][:, cols], func=ACT.Copy, scale=weight)
-            else:
-                nc.gpsimd.tensor_scalar(
-                    out=result[:], in0=diffs[step][:, cols], scalar1=weight, scalar2=0.0, op0=ALU.mult, op1=ALU.add
-                )
-            t0 = tt * N_TILE
-            nc.sync.dma_start(out=out[f * P : (f + 1) * P, t0 + cols.start : t0 + cols.stop], in_=result[:])
-
-        for a in range(PASSES):
-            pieces = [(0, a, c0) for c0 in range(0, N_TILE, PIECE)]
-            for piece in pieces:
-                round_xs(piece)
-                round_x(piece)
-            for name in ("x", "xs"):
-                for piece in pieces:
-                    quantize(name, piece)
-
-        nc.vector.tensor_scalar(out=half_g[:], in0=g_cols[:, 0:F_TILES], scalar1=0.5, scalar2=None, op0=ALU.mult)
-
-        later = [(tt, a, c0) for tt in range(1, T_TILES) for a in range(PASSES) for c0 in range(0, N_TILE, LATER_PIECE)]
-        due = {}
-        for j, piece in enumerate(later):
-            due.setdefault(1 + j * 8 // 5, []).append(piece)
-
-        whole = slice(0, N_TILE)
-        halves = [slice(0, N_TILE // 2), slice(N_TILE // 2, N_TILE)]
-        stored = 0
-        previous = []
-        for step in range(STEPS):
+        def multiply(step):
             if step > 0 and step % F_TILES == 0:
                 for ahead in range(OPEN_AHEAD):
                     pass_a(step + ahead, 0)
@@ -244,31 +197,69 @@ def tile_mix_fm_wgt_kernel(tc, x, v4_words, v4_scales, vs_words, vs_scales, g, o
             if step not in c_sums:
                 pass_c(step, 0)
             pass_c(step, 1)
-            if step == STEPS - 1:
-                break
-            current = due.get(step, [])
+
+        squares = {}
+        diffs = {}
+
+        def square_a(step, cols):
+            if step not in squares:
+                squares[step] = stage.tile([P, T_TILE], F32, name="a_squared")
+            nc.scalar.activation(out=squares[step][:, cols], in_=a_sums[step][:, cols], func=ACT.Square)
+
+        def subtract_c(step, cols):
+            if step not in diffs:
+                diffs[step] = results.tile([P, T_TILE], F32, name="diff", bufs=DIFF_BUFS)
+            nc.vector.tensor_tensor(
+                out=diffs[step][:, cols], in0=squares[step][:, cols], in1=c_sums[step][:, cols], op=ALU.subtract
+            )
+
+        def weigh_and_store(step, cols, on_gpsimd):
+            tt, f = divmod(step, F_TILES)
+            result = results.tile([P, cols.stop - cols.start], F32, name="result")
+            weight = half_g[:, f : f + 1]
+            if on_gpsimd:
+                nc.gpsimd.tensor_scalar(
+                    out=result[:], in0=diffs[step][:, cols], scalar1=weight, scalar2=0.0, op0=ALU.mult, op1=ALU.add
+                )
+            else:
+                nc.vector.tensor_scalar(
+                    out=result[:], in0=diffs[step][:, cols], scalar1=weight, scalar2=None, op0=ALU.mult
+                )
+            t0 = tt * T_TILE
+            nc.sync.dma_start(out=out[f * P : (f + 1) * P, t0 + cols.start : t0 + cols.stop], in_=result[:])
+
+        for n in range(PASSES):
+            first_pieces = [(0, n, c0) for c0 in range(0, T_TILE, PIECE)]
+            for piece in first_pieces:
+                round_xs(piece)
+                round_x(piece)
+            quantize(first_pieces)
+
+        nc.vector.tensor_scalar(out=half_g[:], in0=g_cols[:, 0:F_TILES], scalar1=0.5, scalar2=None, op0=ALU.mult)
+
+        later = [(tt, n, c0) for tt in range(1, T_TILES) for n in range(PASSES) for c0 in range(0, T_TILE, PIECE)]
+        due = {j * PIECE_PACE[0] // PIECE_PACE[1]: [piece] for j, piece in enumerate(later)}
+
+        whole = slice(0, T_TILE)
+        last = STEPS - 1
+        for step in range(last):
+            multiply(step)
             square_a(step, whole)
-            for piece in current:
+            for piece in due.get(step, []):
                 round_xs(piece)
             subtract_c(step, whole)
-            for name in ("x", "xs"):
-                for piece in previous:
-                    quantize(name, piece)
-            engines = EARLY[step % len(EARLY)] if step < SWITCH else LATE[step % len(LATE)]
-            for engine in engines:
-                if stored < step - LAG:
-                    weigh_and_store(stored, whole, engine)
-                    stored = stored + 1
-            for piece in current:
+            quantize(due.get(step - 1, []))
+            if step > 0:
+                weigh_and_store(step - 1, whole, True)
+            for piece in due.get(step, []):
                 round_x(piece)
-            previous = current
 
-        last = STEPS - 1
+        halves = [slice(0, T_TILE // 2), slice(T_TILE // 2, T_TILE)]
+        multiply(last)
         for cols in halves:
             square_a(last, cols)
-        for step in range(stored, last):
-            weigh_and_store(step, whole, "V")
+        weigh_and_store(last - 1, whole, False)
         for cols in halves:
             subtract_c(last, cols)
         for cols in halves:
-            weigh_and_store(last, cols, "V")
+            weigh_and_store(last, cols, False)

from contextlib import ExitStack

import concourse.mybir as mybir
from concourse.masks import make_identity

K, F, T = 1024, 1024, 1536
FLOPS = 2 * 2 * K * F * T

F32 = mybir.dt.float32
BF16 = mybir.dt.bfloat16
I32 = mybir.dt.int32
U32 = mybir.dt.uint32
U8 = mybir.dt.uint8
FP8X4 = mybir.dt.float8_e4m3fn_x4
FP4X4 = mybir.dt.float4_e2m1fn_x4
ALU = mybir.AluOpType
ACT = mybir.ActivationFunctionType

P = 128
PACK = 4
K_PASS = P * PACK
PASSES = K // K_PASS
T_TILE = 512
T_TILES = T // T_TILE
F_TILES = F // P
STEPS = T_TILES * F_TILES
PIECE = 256
RUN = 4
QUADRANT = 32
SCALE_ROWS = 4
FP4_BYTES = 2
FP8_BYTES = 4
VS_FIRST_ROW = 4
PSUM_BANKS = 4
STAGE_BUFS = 4
DIFF_BUFS = 8
PIECE_PACE = (9, 5)
OPEN_AHEAD = 2


def tile_mix_fm_wgt_kernel(tc, x, v4_words, v4_scales, vs_words, vs_scales, g, out):
    nc = tc.nc
    with ExitStack() as ctx:
        keep = ctx.enter_context(tc.tile_pool(name="keep", bufs=1))
        stage = ctx.enter_context(tc.tile_pool(name="stage", bufs=STAGE_BUFS))
        results = ctx.enter_context(tc.tile_pool(name="results", bufs=STEPS + 1))
        psum_a = ctx.enter_context(tc.psum_pool(name="psum_a", bufs=PSUM_BANKS))
        psum_c = ctx.enter_context(tc.psum_pool(name="psum_c", bufs=PSUM_BANKS))
        ctx.enter_context(tc.manual_schedule())

        g_rows = keep.tile([P, P], F32, name="g_rows")
        ident = keep.tile([P, P], F32, name="ident")
        half_g = keep.tile([P, F_TILES], F32, name="half_g")
        v4_plane = keep.tile([P, PASSES * F], U8, name="v4_plane", align_bytes=64)
        vs_plane = keep.tile([P, PASSES * F], U8, name="vs_plane", align_bytes=64)

        nc.gpsimd.memset(g_rows[:], 0.0)
        nc.vector.memset(v4_plane[:].bitcast(U32), 0)
        nc.vector.memset(vs_plane[:].bitcast(U32), 0)
        make_identity(nc, ident[:])

        raw = {}
        v4_codes = {}
        vs_codes = {}

        def load_scales(plane, first_row, scales):
            for r in range(SCALE_ROWS):
                rows = plane[first_row + r : P : QUADRANT, :]
                source = scales[:, r : K_PASS // 32 : SCALE_ROWS, :].rearrange("n q f -> q n f")
                nc.sync.dma_start(
                    out=rows.bitcast(I32).rearrange("q (n f) -> q n f", n=PASSES),
                    in_=source.bitcast(I32),
                )

        def load_x(tt, n, c0, width):
            tile = keep.tile([P, PACK, width], F32, name=f"raw_{tt}_{n}_{c0}")
            t0 = tt * T_TILE + c0
            rows = x[n * K_PASS : (n + 1) * K_PASS, t0 : t0 + width]
            nc.sync.dma_start(out=tile[:], in_=rows.rearrange("(p j) w -> p j w", j=PACK))
            for c in range(0, width, PIECE):
                raw[(tt, n, c0 + c)] = tile[:, :, c : c + PIECE]

        def load_v4(f0, f1):
            row = FP4_BYTES * P
            tile = keep.tile([P, PASSES, row * (f1 - f0)], U8, name=f"v4_{f0}", align_bytes=64)
            source = v4_words[:, :, row * f0 : row * f1].rearrange("n p b -> p n b")
            nc.sync.dma_start(out=tile[:].bitcast(I32), in_=source.bitcast(I32))
            for f in range(f0, f1):
                for n in range(PASSES):
                    v4_codes[(n, f)] = tile[:, n, row * (f - f0) : row * (f - f0 + 1)]

        def load_vs(f0, f1):
            row = FP8_BYTES * P
            tile = keep.tile([P, PASSES, P * (f1 - f0)], U32, name=f"vs_{f0}", align_bytes=64)
            source = vs_words.rearrange("n p f j -> p n (f j)")[:, :, row * f0 : row * f1]
            nc.sync.dma_start(out=tile[:].bitcast(I32), in_=source.bitcast(I32))
            for f in range(f0, f1):
                for n in range(PASSES):
                    vs_codes[(n, f)] = tile[:, n, P * (f - f0) : P * (f - f0 + 1)]

        load_x(0, 0, 0, T_TILE)
        load_x(0, 1, 0, T_TILE)
        nc.sync.dma_start(out=g_rows[0:F_TILES, :], in_=g.rearrange("(c p) -> c p", p=P))
        load_scales(v4_plane, 0, v4_scales)
        load_v4(0, 4)
        load_vs(0, 4)
        load_scales(vs_plane, VS_FIRST_ROW, vs_scales)
        load_x(1, 0, 0, PIECE)
        load_x(1, 0, PIECE, PIECE)
        load_v4(4, 8)
        load_vs(4, 6)
        load_x(1, 1, 0, PIECE)
        load_vs(6, 8)
        load_x(1, 1, PIECE, PIECE)
        load_x(2, 0, 0, T_TILE)
        load_x(2, 1, 0, T_TILE)

        g_cols = psum_a.tile([P, T_TILE], F32, name="a_sum")
        nc.tensor.transpose(g_cols[:, 0:P], g_rows[:], ident[:])

        codes = {}
        planes = {}
        for name in ("x", "xs"):
            for tt in range(T_TILES):
                for n in range(PASSES):
                    codes[(name, tt, n)] = keep.tile([P, T_TILE], U32, name=f"codes_{name}_{tt}_{n}", align_bytes=64)
                    planes[(name, tt, n)] = keep.tile([P, T_TILE], U8, name=f"plane_{name}_{tt}_{n}", align_bytes=64)

        rounded = {}

        def interleaved(piece, tile):
            dst = tile[:].rearrange("p (c i j) -> p c j i", i=RUN, j=PACK)
            src = raw[piece].rearrange("p j (c i) -> p c j i", i=RUN)
            return dst, src

        def round_x(piece):
            tile = stage.tile([P, PACK * PIECE], BF16, name="x_bf16", align_bytes=64)
            dst, src = interleaved(piece, tile)
            nc.vector.tensor_copy(out=dst, in_=src)
            rounded[("x", piece)] = tile

        def round_xs(piece):
            tile = stage.tile([P, PACK * PIECE], BF16, name="xs_bf16", align_bytes=64)
            dst, src = interleaved(piece, tile)
            nc.scalar.activation(out=dst, in_=src, func=ACT.Square)
            rounded[("xs", piece)] = tile

        def quantize(pieces):
            for name in ("x", "xs"):
                for piece in pieces:
                    tt, n, c0 = piece
                    nc.vector.quantize_mx(
                        out=codes[(name, tt, n)][:, c0 : c0 + PIECE].bitcast(FP8X4),
                        scales=planes[(name, tt, n)][:, c0 : c0 + PIECE],
                        in_=rounded[(name, piece)][:],
                    )

        a_sums = {}
        c_sums = {}

        def pass_a(step, n):
            tt, f = divmod(step, F_TILES)
            if n == 0:
                a_sums[step] = psum_a.tile([P, T_TILE], F32, name="a_sum")
            nc.tensor.matmul_mx(
                out=a_sums[step][:],
                lhsT=v4_codes[(n, f)].bitcast(FP4X4),
                lhsT_scale=v4_plane[:, n * F + f * P : n * F + (f + 1) * P],
                rhs=codes[("x", tt, n)][:].bitcast(FP8X4),
                rhs_scale=planes[("x", tt, n)][:],
                start=(n == 0),
                stop=(n == PASSES - 1),
            )

        def pass_c(step, n):
            tt, f = divmod(step, F_TILES)
            if n == 0:
                c_sums[step] = psum_c.tile([P, T_TILE], F32, name="c_sum")
            nc.tensor.matmul_mx(
                out=c_sums[step][:],
                lhsT=vs_codes[(n, f)].bitcast(FP8X4),
                lhsT_scale=vs_plane[VS_FIRST_ROW:P, n * F + f * P : n * F + (f + 1) * P],
                rhs=codes[("xs", tt, n)][:].bitcast(FP8X4),
                rhs_scale=planes[("xs", tt, n)][:],
                start=(n == 0),
                stop=(n == PASSES - 1),
            )

        def multiply(step):
            if step > 0 and step % F_TILES == 0:
                for ahead in range(OPEN_AHEAD):
                    pass_a(step + ahead, 0)
                    pass_c(step + ahead, 0)
            if step not in a_sums:
                pass_a(step, 0)
            pass_a(step, 1)
            if step not in c_sums:
                pass_c(step, 0)
            pass_c(step, 1)

        squares = {}
        diffs = {}

        def square_a(step, cols):
            if step not in squares:
                squares[step] = stage.tile([P, T_TILE], F32, name="a_squared")
            nc.scalar.activation(out=squares[step][:, cols], in_=a_sums[step][:, cols], func=ACT.Square)

        def subtract_c(step, cols):
            if step not in diffs:
                diffs[step] = results.tile([P, T_TILE], F32, name="diff", bufs=DIFF_BUFS)
            nc.vector.tensor_tensor(
                out=diffs[step][:, cols], in0=squares[step][:, cols], in1=c_sums[step][:, cols], op=ALU.subtract
            )

        def weigh_and_store(step, cols, on_gpsimd):
            tt, f = divmod(step, F_TILES)
            result = results.tile([P, cols.stop - cols.start], F32, name="result")
            weight = half_g[:, f : f + 1]
            if on_gpsimd:
                nc.gpsimd.tensor_scalar(
                    out=result[:], in0=diffs[step][:, cols], scalar1=weight, scalar2=0.0, op0=ALU.mult, op1=ALU.add
                )
            else:
                nc.vector.tensor_scalar(
                    out=result[:], in0=diffs[step][:, cols], scalar1=weight, scalar2=None, op0=ALU.mult
                )
            t0 = tt * T_TILE
            nc.sync.dma_start(out=out[f * P : (f + 1) * P, t0 + cols.start : t0 + cols.stop], in_=result[:])

        for n in range(PASSES):
            first_pieces = [(0, n, c0) for c0 in range(0, T_TILE, PIECE)]
            for piece in first_pieces:
                round_xs(piece)
                round_x(piece)
            quantize(first_pieces)

        nc.vector.tensor_scalar(out=half_g[:], in0=g_cols[:, 0:F_TILES], scalar1=0.5, scalar2=None, op0=ALU.mult)

        later = [(tt, n, c0) for tt in range(1, T_TILES) for n in range(PASSES) for c0 in range(0, T_TILE, PIECE)]
        due = {j * PIECE_PACE[0] // PIECE_PACE[1]: [piece] for j, piece in enumerate(later)}

        whole = slice(0, T_TILE)
        last = STEPS - 1
        for step in range(last):
            multiply(step)
            square_a(step, whole)
            for piece in due.get(step, []):
                round_xs(piece)
            subtract_c(step, whole)
            quantize(due.get(step - 1, []))
            if step > 0:
                weigh_and_store(step - 1, whole, True)
            for piece in due.get(step, []):
                round_x(piece)

        halves = [slice(0, T_TILE // 2), slice(T_TILE // 2, T_TILE)]
        multiply(last)
        for cols in halves:
            square_a(last, cols)
        weigh_and_store(last - 1, whole, False)
        for cols in halves:
            subtract_c(last, cols)
        for cols in halves:
            weigh_and_store(last, cols, False)
